import numpy as np
import ml_dtypes


def mxq(x, axis, fmt="e4m3"):
    dtype, down = {"e4m3": (ml_dtypes.float8_e4m3fn, 7), "e5m2": (ml_dtypes.float8_e5m2, 14)}[fmt]
    v = np.moveaxis(np.asarray(x, np.float32).astype(ml_dtypes.bfloat16).astype(np.float64), axis, -1)
    blocks = v.reshape(v.shape[:-1] + (-1, 32))
    amax = np.abs(blocks).max(-1, keepdims=True)
    byte = np.maximum(np.where(amax > 0, np.frexp(amax)[1] - 1 + 127, 0) - down, 1)
    scale = np.exp2(byte - 127.0)
    codes = (blocks / scale).astype(np.float32).astype(dtype).astype(np.float64)
    return np.moveaxis((codes * scale).reshape(v.shape), -1, axis)


WIDE = False


def mx_kscale(k):
    if not WIDE:
        return np.ones(k)
    levels = np.array([10, -10, 5, -5, 0])
    if k % 512:
        return np.exp2(np.random.permutation(np.resize(levels, k // 32))).repeat(32)
    a = np.empty((k // 512, 16))
    for p in range(k // 512):
        a[p, :8] = np.random.permutation(np.resize(levels, 8))
        for g in range(8):
            far = levels[np.abs(levels - a[p, g]) >= 10]
            a[p, g + 8] = far[np.random.randint(len(far))]
    return np.exp2(a.ravel()).repeat(32)


def f64(x):
    return np.asarray(x).astype(np.float64)


def striped(idx):
    return np.tile(idx.reshape(-1, 16).T, (8, 1)).astype(np.uint16)


def unstriped(offs):
    return offs[:16].T.reshape(-1).astype(np.int64)


def pack_weight(w):
    k, n = w.shape
    w = f64(np.asarray(w, np.float32).astype(ml_dtypes.bfloat16)).reshape(k // 32, 32, n)
    amax = np.abs(w).max(1)
    byte = np.clip(np.where(amax > 0, np.frexp(amax)[1] - 1 + 127 - 7, 1), 1, 254)
    scaled = (w * np.exp2(127.0 - byte)[:, None, :]).reshape(k, n).astype(np.float32)
    words = np.ascontiguousarray(scaled.reshape(k // 512, 128, 4, n).transpose(0, 1, 3, 2)).astype(ml_dtypes.float8_e4m3fn).view(np.uint8)
    return words, np.ascontiguousarray(byte.astype(np.uint8).reshape(k // 512, 16, n))


def unpack_weight(words, scales):
    g, p, n, _ = words.shape
    vals = np.ascontiguousarray(words).view(ml_dtypes.float8_e4m3fn).astype(np.float64) * np.repeat(np.exp2(scales.astype(np.float64) - 127.0), 8, axis=1)[..., None]
    return vals.transpose(0, 1, 3, 2).reshape(g * 512, n)


K, T, S, N, H, U = 1024, 2048, 512, 128, 512, 1024


def setup_inputs():
    n = np.random.standard_normal
    s = mx_kscale(K)[:, None]
    u = mx_kscale(H)
    packed_xT = pack_weight(n((K, T)) * s)
    return {
        "x_words": packed_xT[0],
        "x_scales": packed_xT[1],
        "w1": (n((K, H)) / np.sqrt(K) / s).astype(np.float32),
        "w2": (n((K, H)) / np.sqrt(K) / s).astype(np.float32),
        "unit": (np.random.uniform(0.6, 1.4, (H, 1)) * u[:, None]).astype(np.float32),
        "w3": (n((H, N)) / np.sqrt(H) / u[:, None]).astype(np.float32),
        "offs": striped(np.random.permutation(T)[:S]),
        "lef": striped(np.random.permutation(np.concatenate([np.arange(S), np.random.randint(0, S, U - S)]))),
        "rig": striped(np.random.permutation(np.concatenate([np.arange(S), np.random.randint(0, S, U - S)]))),
        "mid": striped(np.random.permutation(np.concatenate([np.arange(S), np.random.randint(0, S, U - S)]))),
    }


def reference(x_words, x_scales, w1, w2, unit, w3, offs, lef, rig, mid):
    xq = unpack_weight(x_words, x_scales)[:, unstriped(offs)]
    y = mxq(f64(w1), 0, "e4m3").T @ xq
    yl = y[:, unstriped(lef)]
    yr = y[:, unstriped(rig)]
    ends = yl + yr
    z1 = mxq(f64(w2), 0, "e4m3").T @ xq
    zm = z1[:, unstriped(mid)]
    ym = y[:, unstriped(mid)]
    hid = f64(unit) * (ends * zm + ym)
    return mxq(f64(w3), 0, "e4m3").T @ mxq(hid, 0, "e4m3")

@@ -1,0 +1,211 @@
+from contextlib import ExitStack
+
+import concourse.mybir as mybir
+
+K, T, S, N, H, U = 1024, 2048, 512, 128, 512, 1024
+FLOPS = 2 * K * H * S * 2 + 2 * H * N * U
+
+F32 = mybir.dt.float32
+BF16 = mybir.dt.bfloat16
+I32 = mybir.dt.int32
+U32 = mybir.dt.uint32
+U16 = mybir.dt.uint16
+U8 = mybir.dt.uint8
+FP8X4 = mybir.dt.float8_e4m3fn_x4
+COPY = mybir.ActivationFunctionType.Copy
+ADD = mybir.AluOpType.add
+MULT = mybir.AluOpType.mult
+
+P = 128
+PACK = 4
+PASSES = K // (P * PACK)
+CHUNKS = ((0, 384), (384, 384), (768, 256))
+
+
+def tile_picked_ybrdgep_mul_p_kernel(tc, x_words, x_scales, w1, w2, unit, w3, offs, lef, rig, mid, out):
+    nc = tc.nc
+    with ExitStack() as ctx:
+        sb = ctx.enter_context(tc.tile_pool(name="sb", bufs=1))
+        ps = ctx.enter_context(tc.psum_pool(name="ps", bufs=1))
+
+        def tile(shape, dtype, name):
+            return sb.tile(shape, dtype, name=name, align_bytes=64)
+
+        def load_list(src, name):
+            t = tile([P, src.shape[1]], U16, name)
+            nc.sync.dma_start(t[:], src)
+            return t
+
+        def load_words(o):
+            t = tile([P, T], U32, "xw%d" % o)
+            nc.sync.dma_start(t[:].bitcast(I32), x_words[o].rearrange("p n r -> p (n r)").bitcast(I32))
+            return t
+
+        def load_rows(w, o, c0, width, name):
+            t = tile([P, PACK, width], F32, name)
+            nc.sync.dma_start(t[:], w[o * 512 : (o + 1) * 512, c0 : c0 + width].rearrange("(p j) c -> p j c", j=PACK))
+            return t
+
+        stage = tile([P, T], U8, "stage")
+
+        w1_0 = load_rows(w1, 0, 0, 512, "w1_0")
+        offs_t = load_list(offs, "offs_t")
+        for q in range(4):
+            nc.sync.dma_start(stage[32 * q : 32 * q + 8, :].bitcast(I32), x_scales[:, 4 * q : 4 * q + 4, :].bitcast(I32))
+        xw1 = load_words(1)
+        xw0 = load_words(0)
+        w1_1a = load_rows(w1, 1, 0, 256, "w1_1a")
+        w1_1b = load_rows(w1, 1, 256, 256, "w1_1b")
+        unit_t = tile([P, PACK], F32, "unit_t")
+        nc.sync.dma_start(unit_t[:], unit.rearrange("(p t) o -> p (t o)", t=PACK))
+        lef_t = load_list(lef, "lef_t")
+        rig_t = load_list(rig, "rig_t")
+        mid_t = load_list(mid, "mid_t")
+        w2_0 = load_rows(w2, 0, 0, 512, "w2_0")
+        w2_1 = load_rows(w2, 1, 0, 512, "w2_1")
+        w3_t = load_rows(w3, 0, 0, N, "w3_t")
+
+        def gather_words(win, o):
+            g = tile([P, S], U32, "xg%d" % o)
+            nc.vector.tensor_copy(g[:], win[:].indirect(offs_t[:]))
+            return g
+
+        def deal(copy, raw, name, t0=0, nt=PACK):
+            m = raw.shape[2] // PACK
+            b = tile([P, nt, m, PACK], BF16, name)
+            copy(b[:].rearrange("p t m j -> p m j t"), raw[:].rearrange("p j (m t) -> p m j t", t=PACK)[:, :, :, t0 : t0 + nt])
+            return b
+
+        def planes(width, name):
+            return tile([P, width], U32, name + "_c"), tile([P, width], U8, name + "_s")
+
+        def quant(cs, c0, src):
+            n = src.shape[1] // PACK
+            nc.vector.quantize_mx(cs[0][:, c0 : c0 + n].bitcast(FP8X4), cs[1][:, c0 : c0 + n], src)
+
+        def first_product(bank, wq, xg, o, t):
+            cols = slice(t * P, (t + 1) * P)
+            nc.tensor.matmul_mx(bank[:], lhsT=wq[0][:, cols].bitcast(FP8X4), lhsT_scale=wq[1][:, cols],
+                                rhs=xg[:].bitcast(FP8X4), rhs_scale=xs[4 * o : P, :],
+                                start=(o == 0), stop=(o == PASSES - 1))
+
+        xs_win = tile([P, T], U8, "xs_win")
+        nc.vector.memset(xs_win[:].bitcast(I32), 0)
+        b = deal(nc.scalar.copy, w1_0, "w1_0b")
+        for q in range(4):
+            rows = slice(32 * q, 32 * q + 8)
+            nc.vector.tensor_copy(xs_win[rows, :].bitcast(I32), stage[rows, :].bitcast(I32))
+        xs = tile([P, S], U8, "xs")
+        nc.vector.tensor_copy(xs[:], xs_win[:].indirect(offs_t[:]))
+        xg1 = gather_words(xw1, 1)
+        w1q0 = planes(H, "w1q0")
+        quant(w1q0, 0, b[:].rearrange("p t m j -> p (t m j)"))
+        xg0 = gather_words(xw0, 0)
+        ybank = [ps.tile([P, S], F32, name="bank%d" % t) for t in range(PACK)]
+        for t in range(PACK):
+            first_product(ybank[t], w1q0, xg0, 0, t)
+        w1q1 = planes(H, "w1q1")
+        ba = deal(nc.scalar.copy, w1_1a, "w1_1ab")
+        bb = [deal(nc.vector.tensor_copy, w1_1b, "w1_1b0", 0, 2), deal(nc.scalar.copy, w1_1b, "w1_1b1", 2, 2)]
+        y = [tile([P, S], F32, "y%d" % t) for t in range(PACK)]
+        for t in range(PACK):
+            quant(w1q1, t * P, ba[:, t, :, :].rearrange("p m j -> p (m j)"))
+            quant(w1q1, t * P + 64, bb[t // 2][:, t % 2, :, :].rearrange("p m j -> p (m j)"))
+            first_product(ybank[t], w1q1, xg1, 1, t)
+        for t in range(PACK):
+            if t != 1:
+                nc.scalar.activation(y[t][:], ybank[t][:], COPY, scale=unit_t[:, t : t + 1])
+            else:
+                nc.vector.tensor_scalar(y[t][:], ybank[t][:], unit_t[:, t : t + 1], None, MULT)
+
+        def entries(lst, c):
+            c0, n = CHUNKS[c]
+            return lst[:, c0 // 16 : (c0 + n) // 16]
+
+        left = [tile([P, PACK, n], F32, "left%d" % c) for c, (c0, n) in enumerate(CHUNKS)]
+        ends = [tile([P, PACK, n], F32, "ends%d" % c) for c, (c0, n) in enumerate(CHUNKS)]
+        prod = [tile([P, PACK, n], F32, "prod%d" % c) for c, (c0, n) in enumerate(CHUNKS)]
+        load = [tile([P, PACK, n], F32, "load%d" % c) for c, (c0, n) in enumerate(CHUNKS)]
+
+        def g_left(c):
+            for t in range(PACK):
+                nc.scalar.activation(left[c][:, t, :], y[t][:].indirect(entries(lef_t, c)), COPY)
+
+        def g_ends(c):
+            for t in range(PACK):
+                nc.vector.tensor_tensor(ends[c][:, t, :], y[t][:].indirect(entries(rig_t, c)), left[c][:, t, :], ADD)
+
+        def g_load(c):
+            for t in range(PACK):
+                nc.scalar.activation(load[c][:, t, :], y[t][:].indirect(entries(mid_t, c)), COPY)
+
+        def g_prod(c):
+            for t in range(PACK):
+                nc.vector.tensor_tensor(prod[c][:, t, :], z[t][:].indirect(entries(mid_t, c)), ends[c][:, t, :], MULT)
+
+        def g_stiff(c):
+            st = tile([P, PACK, CHUNKS[c][1]], F32, "stiff")
+            for t in range(PACK):
+                nc.scalar.activation(st[:, t, :], z[t][:].indirect(entries(mid_t, c)), COPY)
+            return st
+
+        def finish(c, a, n):
+            hid = tile([P, n, PACK], BF16, "hid%d_%d" % (c, a))
+            nc.vector.tensor_tensor(hid[:].rearrange("p (c i) t -> p c t i", i=4),
+                                    prod[c][:, :, a : a + n].rearrange("p t (c i) -> p c t i", i=4),
+                                    load[c][:, :, a : a + n].rearrange("p t (c i) -> p c t i", i=4), ADD)
+            return hid
+
+        def last_product(c, a, n, hid, b):
+            c0 = CHUNKS[c][0] + a
+            hq = planes(n, "hq%d_%d" % (c, a))
+            quant(hq, 0, hid[:].rearrange("p n t -> p (n t)"))
+            bank = ps.tile([P, S], F32, name="bank%d" % b)
+            for a in range(0, n, 256):
+                cols = slice(a, min(a + 256, n))
+                nc.tensor.matmul_mx(bank[:, cols], lhsT=w3q[0][:].bitcast(FP8X4), lhsT_scale=w3q[1][:],
+                                    rhs=hq[0][:, cols].bitcast(FP8X4), rhs_scale=hq[1][:, cols], start=True, stop=True)
+            res = tile([P, n], F32, "res%d" % b)
+            nc.scalar.copy(res[:], bank[:, 0:n])
+            nc.sync.dma_start(out[:, c0 : c0 + n], res[:])
+
+        zbank = [ps.tile([P, S], F32, name="bank%d" % (PACK + t)) for t in range(PACK)]
+        z = [tile([P, S], F32, "z%d" % t) for t in range(PACK)]
+
+        b20 = deal(nc.vector.tensor_copy, w2_0, "w2_0b")
+        g_left(0)
+        w2q0 = planes(H, "w2q0")
+        quant(w2q0, 0, b20[:].rearrange("p t m j -> p (t m j)"))
+        for t in range(PACK):
+            first_product(zbank[t], w2q0, xg0, 0, t)
+        b21 = deal(nc.vector.tensor_copy, w2_1, "w2_1b")
+        w2q1 = planes(H, "w2q1")
+        quant(w2q1, 0, b21[:].rearrange("p t m j -> p (t m j)"))
+        for t in range(PACK):
+            first_product(zbank[t], w2q1, xg1, 1, t)
+        for t in range(PACK):
+            nc.scalar.copy(z[t][:], zbank[t][:])
+        g_ends(0)
+        g_left(1)
+        g_ends(1)
+        g_load(0)
+        g_prod(0)
+        w3b = tile([P, N, PACK], BF16, "w3b")
+        nc.scalar.copy(w3b[:].rearrange("p (c i) j -> p c j i", i=4), w3_t[:].rearrange("p j (c i) -> p c j i", i=4))
+        w3q = planes(N, "w3q")
+        quant(w3q, 0, w3b[:].rearrange("p n j -> p (n j)"))
+        g_left(2)
+        hid0 = finish(0, 0, 384)
+        g_ends(2)
+        g_load(1)
+        last_product(0, 0, 384, hid0, 0)
+        g_prod(1)
+        hid1 = finish(1, 0, 384)
+        st = g_stiff(2)
+        g_load(2)
+        nc.vector.tensor_tensor(prod[2][:], st[:], ends[2][:], MULT)
+        last_product(1, 0, 384, hid1, 1)
+        hid2 = finish(2, 0, 128)
+        hid3 = finish(2, 128, 128)
+        last_product(2, 0, 128, hid2, 2)
+        last_product(2, 128, 128, hid3, 3)

@@ -19,7 +19,9 @@ MULT = mybir.AluOpType.mult
 P = 128
 PACK = 4
 PASSES = K // (P * PACK)
-CHUNKS = ((0, 384), (384, 384), (768, 256))
+CHUNKS = ((0, 768), (768, 256))
+Y_WIN = U + 16
+Z_WIN = 768 + 16
 
 
 def tile_picked_ybrdgep_mul_p_kernel(tc, x_words, x_scales, w1, w2, unit, w3, offs, lef, rig, mid, out):
@@ -28,8 +30,8 @@ def tile_picked_ybrdgep_mul_p_kernel(tc, x_words, x_scales, w1, w2, unit, w3, of
         sb = ctx.enter_context(tc.tile_pool(name="sb", bufs=1))
         ps = ctx.enter_context(tc.psum_pool(name="ps", bufs=1))
 
-        def tile(shape, dtype, name):
-            return sb.tile(shape, dtype, name=name, align_bytes=64)
+        def tile(shape, dtype, name, tag=None):
+            return sb.tile(shape, dtype, name=name, tag=tag or name, align_bytes=64)
 
         def load_list(src, name):
             t = tile([P, src.shape[1]], U16, name)
@@ -48,12 +50,13 @@ def tile_picked_ybrdgep_mul_p_kernel(tc, x_words, x_scales, w1, w2, unit, w3, of
 
         stage = tile([P, T], U8, "stage")
 
-        w1_0 = load_rows(w1, 0, 0, 512, "w1_0")
         offs_t = load_list(offs, "offs_t")
         for q in range(4):
-            nc.sync.dma_start(stage[32 * q : 32 * q + 8, :].bitcast(I32), x_scales[:, 4 * q : 4 * q + 4, :].bitcast(I32))
-        xw1 = load_words(1)
+            queue = nc.sync if q < 2 else nc.scalar
+            queue.dma_start(stage[32 * q : 32 * q + 8, :].bitcast(I32), x_scales[:, 4 * q : 4 * q + 4, :].bitcast(I32))
+        w1_0 = load_rows(w1, 0, 0, 512, "w1_0")
         xw0 = load_words(0)
+        xw1 = load_words(1)
         w1_1a = load_rows(w1, 1, 0, 256, "w1_1a")
         w1_1b = load_rows(w1, 1, 256, 256, "w1_1b")
         unit_t = tile([P, PACK], F32, "unit_t")
@@ -89,6 +92,11 @@ def tile_picked_ybrdgep_mul_p_kernel(tc, x_words, x_scales, w1, w2, unit, w3, of
                                 rhs=xg[:].bitcast(FP8X4), rhs_scale=xs[4 * o : P, :],
                                 start=(o == 0), stop=(o == PASSES - 1))
 
+        y = [tile([P, Y_WIN], F32, "y%d" % t) for t in range(PACK)]
+        z = [tile([P, Z_WIN], F32, "z%d" % t) for t in range(PACK)]
+        for t in range(PACK):
+            nc.gpsimd.memset(y[t][:, S:], 0.0)
+            nc.gpsimd.memset(z[t][:, S:], 0.0)
         xs_win = tile([P, T], U8, "xs_win")
         nc.vector.memset(xs_win[:].bitcast(I32), 0)
         b = deal(nc.scalar.copy, w1_0, "w1_0b")
@@ -97,43 +105,39 @@ def tile_picked_ybrdgep_mul_p_kernel(tc, x_words, x_scales, w1, w2, unit, w3, of
             nc.vector.tensor_copy(xs_win[rows, :].bitcast(I32), stage[rows, :].bitcast(I32))
         xs = tile([P, S], U8, "xs")
         nc.vector.tensor_copy(xs[:], xs_win[:].indirect(offs_t[:]))
-        xg1 = gather_words(xw1, 1)
+        xg0 = gather_words(xw0, 0)
         w1q0 = planes(H, "w1q0")
         quant(w1q0, 0, b[:].rearrange("p t m j -> p (t m j)"))
-        xg0 = gather_words(xw0, 0)
         ybank = [ps.tile([P, S], F32, name="bank%d" % t) for t in range(PACK)]
         for t in range(PACK):
             first_product(ybank[t], w1q0, xg0, 0, t)
+        xg1 = gather_words(xw1, 1)
         w1q1 = planes(H, "w1q1")
-        ba = deal(nc.scalar.copy, w1_1a, "w1_1ab")
-        bb = [deal(nc.vector.tensor_copy, w1_1b, "w1_1b0", 0, 2), deal(nc.scalar.copy, w1_1b, "w1_1b1", 2, 2)]
-        y = [tile([P, S], F32, "y%d" % t) for t in range(PACK)]
+        ba = [deal(nc.vector.tensor_copy, w1_1a, "w1_1a0", 0, 2), deal(nc.scalar.copy, w1_1a, "w1_1a1", 2, 2)]
         for t in range(PACK):
-            quant(w1q1, t * P, ba[:, t, :, :].rearrange("p m j -> p (m j)"))
+            quant(w1q1, t * P, ba[t // 2][:, t % 2, :, :].rearrange("p m j -> p (m j)"))
+        bb = [deal(nc.vector.tensor_copy, w1_1b, "w1_1b0", 0, 2), deal(nc.scalar.copy, w1_1b, "w1_1b1", 2, 2)]
+        for t in range(PACK):
             quant(w1q1, t * P + 64, bb[t // 2][:, t % 2, :, :].rearrange("p m j -> p (m j)"))
             first_product(ybank[t], w1q1, xg1, 1, t)
         for t in range(PACK):
             if t != 1:
-                nc.scalar.activation(y[t][:], ybank[t][:], COPY, scale=unit_t[:, t : t + 1])
+                nc.scalar.activation(y[t][:, :S], ybank[t][:], COPY, scale=unit_t[:, t : t + 1])
             else:
-                nc.vector.tensor_scalar(y[t][:], ybank[t][:], unit_t[:, t : t + 1], None, MULT)
+                nc.vector.tensor_scalar(y[t][:, :S], ybank[t][:], unit_t[:, t : t + 1], None, MULT)
 
         def entries(lst, c):
             c0, n = CHUNKS[c]
             return lst[:, c0 // 16 : (c0 + n) // 16]
 
-        left = [tile([P, PACK, n], F32, "left%d" % c) for c, (c0, n) in enumerate(CHUNKS)]
-        ends = [tile([P, PACK, n], F32, "ends%d" % c) for c, (c0, n) in enumerate(CHUNKS)]
+        left = tile([P, PACK, U], F32, "left")
         prod = [tile([P, PACK, n], F32, "prod%d" % c) for c, (c0, n) in enumerate(CHUNKS)]
-        load = [tile([P, PACK, n], F32, "load%d" % c) for c, (c0, n) in enumerate(CHUNKS)]
 
-        def g_left(c):
-            for t in range(PACK):
-                nc.scalar.activation(left[c][:, t, :], y[t][:].indirect(entries(lef_t, c)), COPY)
+        def g_left(t):
+            nc.scalar.activation(left[:, t, :], y[t][:].indirect(lef_t[:]), COPY)
 
-        def g_ends(c):
-            for t in range(PACK):
-                nc.vector.tensor_tensor(ends[c][:, t, :], y[t][:].indirect(entries(rig_t, c)), left[c][:, t, :], ADD)
+        def g_ends(t):
+            nc.vector.tensor_tensor(ends[:, t, :], y[t][:].indirect(rig_t[:]), left[:, t, :], ADD)
 
         def g_load(c):
             for t in range(PACK):
@@ -141,7 +145,7 @@ def tile_picked_ybrdgep_mul_p_kernel(tc, x_words, x_scales, w1, w2, unit, w3, of
 
         def g_prod(c):
             for t in range(PACK):
-                nc.vector.tensor_tensor(prod[c][:, t, :], z[t][:].indirect(entries(mid_t, c)), ends[c][:, t, :], MULT)
+                nc.vector.tensor_tensor(prod[c][:, t, :], z[t][:].indirect(entries(mid_t, c)), ends[:, t, CHUNKS[c][0] : CHUNKS[c][0] + CHUNKS[c][1]], MULT)
 
         def g_stiff(c):
             st = tile([P, PACK, CHUNKS[c][1]], F32, "stiff")
@@ -161,8 +165,8 @@ def tile_picked_ybrdgep_mul_p_kernel(tc, x_words, x_scales, w1, w2, unit, w3, of
             hq = planes(n, "hq%d_%d" % (c, a))
             quant(hq, 0, hid[:].rearrange("p n t -> p (n t)"))
             bank = ps.tile([P, S], F32, name="bank%d" % b)
-            for a in range(0, n, 256):
-                cols = slice(a, min(a + 256, n))
+            for a in range(0, n, 512):
+                cols = slice(a, min(a + 512, n))
                 nc.tensor.matmul_mx(bank[:, cols], lhsT=w3q[0][:].bitcast(FP8X4), lhsT_scale=w3q[1][:],
                                     rhs=hq[0][:, cols].bitcast(FP8X4), rhs_scale=hq[1][:, cols], start=True, stop=True)
             res = tile([P, n], F32, "res%d" % b)
@@ -170,42 +174,39 @@ def tile_picked_ybrdgep_mul_p_kernel(tc, x_words, x_scales, w1, w2, unit, w3, of
             nc.sync.dma_start(out[:, c0 : c0 + n], res[:])
 
         zbank = [ps.tile([P, S], F32, name="bank%d" % (PACK + t)) for t in range(PACK)]
-        z = [tile([P, S], F32, "z%d" % t) for t in range(PACK)]
 
         b20 = deal(nc.vector.tensor_copy, w2_0, "w2_0b")
-        g_left(0)
         w2q0 = planes(H, "w2q0")
         quant(w2q0, 0, b20[:].rearrange("p t m j -> p (t m j)"))
         for t in range(PACK):
             first_product(zbank[t], w2q0, xg0, 0, t)
-        b21 = deal(nc.vector.tensor_copy, w2_1, "w2_1b")
-        w2q1 = planes(H, "w2q1")
-        quant(w2q1, 0, b21[:].rearrange("p t m j -> p (t m j)"))
+        b21 = [deal(nc.vector.tensor_copy, w2_1, "w2_1b%d" % h, 2 * h, 2) for h in range(2)]
+        w2q1 = [planes(2 * P, "w2q1%d" % h) for h in range(2)]
+        for h in range(2):
+            quant(w2q1[h], 0, b21[h][:].rearrange("p t m j -> p (t m j)"))
         for t in range(PACK):
-            first_product(zbank[t], w2q1, xg1, 1, t)
+            first_product(zbank[t], w2q1[t // 2], xg1, 1, t % 2)
         for t in range(PACK):
-            nc.scalar.copy(z[t][:], zbank[t][:])
-        g_ends(0)
-        g_left(1)
-        g_ends(1)
+            nc.scalar.copy(z[t][:, :S], zbank[t][:])
+        ends = tile([P, PACK, U], F32, "ends", "w2_1b1")
+        load = [tile([P, PACK, n], F32, "load%d" % c, ("w2q11_c", "w2q11_s")[c]) for c, (c0, n) in enumerate(CHUNKS)]
+        for t in range(PACK):
+            g_left(t)
+            g_ends(t)
         g_load(0)
         g_prod(0)
-        w3b = tile([P, N, PACK], BF16, "w3b")
+        w3b = tile([P, N, PACK], BF16, "w3b", "w2q10_c")
         nc.scalar.copy(w3b[:].rearrange("p (c i) j -> p c j i", i=4), w3_t[:].rearrange("p j (c i) -> p c j i", i=4))
         w3q = planes(N, "w3q")
         quant(w3q, 0, w3b[:].rearrange("p n j -> p (n j)"))
-        g_left(2)
-        hid0 = finish(0, 0, 384)
-        g_ends(2)
+        st = g_stiff(1)
+        hid0 = finish(0, 0, 512)
+        hid1 = finish(0, 512, 256)
+        last_product(0, 0, 512, hid0, 0)
+        last_product(0, 512, 256, hid1, 1)
         g_load(1)
-        last_product(0, 0, 384, hid0, 0)
-        g_prod(1)
-        hid1 = finish(1, 0, 384)
-        st = g_stiff(2)
-        g_load(2)
-        nc.vector.tensor_tensor(prod[2][:], st[:], ends[2][:], MULT)
-        last_product(1, 0, 384, hid1, 1)
-        hid2 = finish(2, 0, 128)
-        hid3 = finish(2, 128, 128)
-        last_product(2, 0, 128, hid2, 2)
-        last_product(2, 128, 128, hid3, 3)
+        nc.vector.tensor_tensor(prod[1][:], st[:], ends[:, :, CHUNKS[1][0] :], MULT)
+        hid2 = finish(1, 0, 128)
+        hid3 = finish(1, 128, 128)
+        last_product(1, 0, 128, hid2, 2)
+        last_product(1, 128, 128, hid3, 3)

@@ -19,9 +19,11 @@ MULT = mybir.AluOpType.mult
 P = 128
 PACK = 4
 PASSES = K // (P * PACK)
-CHUNKS = ((0, 768), (768, 256))
+ZS = 704
+CHUNKS = ((0, ZS), (ZS, U - ZS))
+LOADS = ((0, 640), (640, 256), (896, 128))
 Y_WIN = U + 16
-Z_WIN = 768 + 16
+Z_WIN = ZS + 16
 
 
 def tile_picked_ybrdgep_mul_p_kernel(tc, x_words, x_scales, w1, w2, unit, w3, offs, lef, rig, mid, out):
@@ -64,8 +66,7 @@ def tile_picked_ybrdgep_mul_p_kernel(tc, x_words, x_scales, w1, w2, unit, w3, of
         lef_t = load_list(lef, "lef_t")
         rig_t = load_list(rig, "rig_t")
         mid_t = load_list(mid, "mid_t")
-        w2_0 = load_rows(w2, 0, 0, 512, "w2_0")
-        w2_1 = load_rows(w2, 1, 0, 512, "w2_1")
+        w2_h = [[load_rows(w2, o, 256 * h, 256, "w2_%d%d" % (o, h)) for h in range(2)] for o in range(PASSES)]
         w3_t = load_rows(w3, 0, 0, N, "w3_t")
 
         def gather_words(win, o):
@@ -121,7 +122,7 @@ def tile_picked_ybrdgep_mul_p_kernel(tc, x_words, x_scales, w1, w2, unit, w3, of
             quant(w1q1, t * P + 64, bb[t // 2][:, t % 2, :, :].rearrange("p m j -> p (m j)"))
             first_product(ybank[t], w1q1, xg1, 1, t)
         for t in range(PACK):
-            if t != 1:
+            if t != 7:
                 nc.scalar.activation(y[t][:, :S], ybank[t][:], COPY, scale=unit_t[:, t : t + 1])
             else:
                 nc.vector.tensor_scalar(y[t][:, :S], ybank[t][:], unit_t[:, t : t + 1], None, MULT)
@@ -131,7 +132,7 @@ def tile_picked_ybrdgep_mul_p_kernel(tc, x_words, x_scales, w1, w2, unit, w3, of
             return lst[:, c0 // 16 : (c0 + n) // 16]
 
         left = tile([P, PACK, U], F32, "left")
-        prod = [tile([P, PACK, n], F32, "prod%d" % c) for c, (c0, n) in enumerate(CHUNKS)]
+        prod = tile([P, PACK, U], F32, "prod")
 
         def g_left(t):
             nc.scalar.activation(left[:, t, :], y[t][:].indirect(lef_t[:]), COPY)
@@ -140,12 +141,13 @@ def tile_picked_ybrdgep_mul_p_kernel(tc, x_words, x_scales, w1, w2, unit, w3, of
             nc.vector.tensor_tensor(ends[:, t, :], y[t][:].indirect(rig_t[:]), left[:, t, :], ADD)
 
         def g_load(c):
+            c0, n = LOADS[c]
             for t in range(PACK):
-                nc.scalar.activation(load[c][:, t, :], y[t][:].indirect(entries(mid_t, c)), COPY)
+                nc.scalar.activation(load[c][:, t, :], y[t][:].indirect(mid_t[:, c0 // 16 : (c0 + n) // 16]), COPY)
 
         def g_prod(c):
             for t in range(PACK):
-                nc.vector.tensor_tensor(prod[c][:, t, :], z[t][:].indirect(entries(mid_t, c)), ends[:, t, CHUNKS[c][0] : CHUNKS[c][0] + CHUNKS[c][1]], MULT)
+                nc.vector.tensor_tensor(prod[:, t, :ZS], z[t][:].indirect(entries(mid_t, c)), ends[:, t, CHUNKS[c][0] : CHUNKS[c][0] + CHUNKS[c][1]], MULT)
 
         def g_stiff(c):
             st = tile([P, PACK, CHUNKS[c][1]], F32, "stiff")
@@ -153,20 +155,20 @@ def tile_picked_ybrdgep_mul_p_kernel(tc, x_words, x_scales, w1, w2, unit, w3, of
                 nc.scalar.activation(st[:, t, :], z[t][:].indirect(entries(mid_t, c)), COPY)
             return st
 
-        def finish(c, a, n):
+        def finish(c, a, n, ld):
             hid = tile([P, n, PACK], BF16, "hid%d_%d" % (c, a))
             nc.vector.tensor_tensor(hid[:].rearrange("p (c i) t -> p c t i", i=4),
-                                    prod[c][:, :, a : a + n].rearrange("p t (c i) -> p c t i", i=4),
-                                    load[c][:, :, a : a + n].rearrange("p t (c i) -> p c t i", i=4), ADD)
+                                    prod[:, :, a : a + n].rearrange("p t (c i) -> p c t i", i=4),
+                                    ld.rearrange("p t (c i) -> p c t i", i=4), ADD)
             return hid
 
         def last_product(c, a, n, hid, b):
-            c0 = CHUNKS[c][0] + a
+            c0 = a
             hq = planes(n, "hq%d_%d" % (c, a))
             quant(hq, 0, hid[:].rearrange("p n t -> p (n t)"))
             bank = ps.tile([P, S], F32, name="bank%d" % b)
-            for a in range(0, n, 512):
-                cols = slice(a, min(a + 512, n))
+            for a in range(0, n, 256):
+                cols = slice(a, min(a + 256, n))
                 nc.tensor.matmul_mx(bank[:, cols], lhsT=w3q[0][:].bitcast(FP8X4), lhsT_scale=w3q[1][:],
                                     rhs=hq[0][:, cols].bitcast(FP8X4), rhs_scale=hq[1][:, cols], start=True, stop=True)
             res = tile([P, n], F32, "res%d" % b)
@@ -175,38 +177,49 @@ def tile_picked_ybrdgep_mul_p_kernel(tc, x_words, x_scales, w1, w2, unit, w3, of
 
         zbank = [ps.tile([P, S], F32, name="bank%d" % (PACK + t)) for t in range(PACK)]
 
-        b20 = deal(nc.vector.tensor_copy, w2_0, "w2_0b")
+        def deal_halves(o):
+            b = tile([P, PACK, P, PACK], BF16, "w2b%d" % o)
+            for h in range(2):
+                nc.vector.tensor_copy(b[:, :, 64 * h : 64 * h + 64, :].rearrange("p t m j -> p m j t"),
+                                      w2_h[o][h][:].rearrange("p j (m t) -> p m j t", t=PACK))
+            return b
+
+        b20 = deal_halves(0)
         w2q0 = planes(H, "w2q0")
         quant(w2q0, 0, b20[:].rearrange("p t m j -> p (t m j)"))
         for t in range(PACK):
             first_product(zbank[t], w2q0, xg0, 0, t)
-        b21 = [deal(nc.vector.tensor_copy, w2_1, "w2_1b%d" % h, 2 * h, 2) for h in range(2)]
+        b21 = deal_halves(1)
         w2q1 = [planes(2 * P, "w2q1%d" % h) for h in range(2)]
         for h in range(2):
-            quant(w2q1[h], 0, b21[h][:].rearrange("p t m j -> p (t m j)"))
+            quant(w2q1[h], 0, b21[:, 2 * h : 2 * h + 2, :, :].rearrange("p t m j -> p (t m j)"))
         for t in range(PACK):
             first_product(zbank[t], w2q1[t // 2], xg1, 1, t % 2)
         for t in range(PACK):
             nc.scalar.copy(z[t][:, :S], zbank[t][:])
-        ends = tile([P, PACK, U], F32, "ends", "w2_1b1")
-        load = [tile([P, PACK, n], F32, "load%d" % c, ("w2q11_c", "w2q11_s")[c]) for c, (c0, n) in enumerate(CHUNKS)]
+        ends = tile([P, PACK, U], F32, "ends", "w2b1")
+        load_head = tile([P, PACK, 640], F32, "load_head", "w2q11_c")
+        load_tail = tile([P, PACK * 384], F32, "load_tail", "w2q11_s")
+        load = [load_head[:], load_tail[:, : PACK * 256].rearrange("p (t n) -> p t n", t=PACK),
+                load_tail[:, PACK * 256 :].rearrange("p (t n) -> p t n", t=PACK)]
         for t in range(PACK):
             g_left(t)
             g_ends(t)
-        g_load(0)
-        g_prod(0)
         w3b = tile([P, N, PACK], BF16, "w3b", "w2q10_c")
         nc.scalar.copy(w3b[:].rearrange("p (c i) j -> p c j i", i=4), w3_t[:].rearrange("p j (c i) -> p c j i", i=4))
+        g_load(0)
+        g_prod(0)
         w3q = planes(N, "w3q")
         quant(w3q, 0, w3b[:].rearrange("p n j -> p (n j)"))
         st = g_stiff(1)
-        hid0 = finish(0, 0, 512)
-        hid1 = finish(0, 512, 256)
-        last_product(0, 0, 512, hid0, 0)
-        last_product(0, 512, 256, hid1, 1)
+        hid0 = finish(0, 0, 384, load[0][:, :, 0:384])
+        hid1 = finish(0, 384, 256, load[0][:, :, 384:640])
+        last_product(0, 0, 384, hid0, 0)
+        last_product(0, 384, 256, hid1, 1)
         g_load(1)
-        nc.vector.tensor_tensor(prod[1][:], st[:], ends[:, :, CHUNKS[1][0] :], MULT)
-        hid2 = finish(1, 0, 128)
-        hid3 = finish(1, 128, 128)
-        last_product(1, 0, 128, hid2, 2)
-        last_product(1, 128, 128, hid3, 3)
+        g_load(2)
+        nc.vector.tensor_tensor(prod[:, :, ZS:], st[:], ends[:, :, CHUNKS[1][0] :], MULT)
+        hid2 = finish(1, 640, 256, load[1])
+        hid3 = finish(1, 896, 128, load[2])
+        last_product(1, 640, 256, hid2, 2)
+        last_product(1, 896, 128, hid3, 3)

@@ -18,12 +18,10 @@ MULT = mybir.AluOpType.mult
 
 P = 128
 PACK = 4
-PASSES = K // (P * PACK)
-ZS = 704
-CHUNKS = ((0, ZS), (ZS, U - ZS))
-LOADS = ((0, 640), (640, 256), (896, 128))
-Y_WIN = U + 16
-Z_WIN = ZS + 16
+K_PASS = P * PACK
+WINDOW = U + 16
+PIECES = ((0, 512), (512, 256), (768, 128), (896, 128))
+Y_ON_VECTOR = (1,)
 
 
 def tile_picked_ybrdgep_mul_p_kernel(tc, x_words, x_scales, w1, w2, unit, w3, offs, lef, rig, mid, out):
@@ -36,190 +34,163 @@ def tile_picked_ybrdgep_mul_p_kernel(tc, x_words, x_scales, w1, w2, unit, w3, of
             return sb.tile(shape, dtype, name=name, tag=tag or name, align_bytes=64)
 
         def load_list(src, name):
-            t = tile([P, src.shape[1]], U16, name)
-            nc.sync.dma_start(t[:], src)
-            return t
+            dst = tile([P, src.shape[1]], U16, name)
+            nc.sync.dma_start(dst[:], src)
+            return dst
 
         def load_words(o):
-            t = tile([P, T], U32, "xw%d" % o)
-            nc.sync.dma_start(t[:].bitcast(I32), x_words[o].rearrange("p n r -> p (n r)").bitcast(I32))
-            return t
+            dst = tile([P, T], U32, "x_window%d" % o)
+            nc.sync.dma_start(dst[:].bitcast(I32), x_words[o].rearrange("p n r -> p (n r)").bitcast(I32))
+            return dst
 
-        def load_rows(w, o, c0, width, name):
-            t = tile([P, PACK, width], F32, name)
-            nc.sync.dma_start(t[:], w[o * 512 : (o + 1) * 512, c0 : c0 + width].rearrange("(p j) c -> p j c", j=PACK))
-            return t
+        def load_rows(w, o, name):
+            dst = tile([P, PACK, w.shape[1]], F32, name)
+            nc.sync.dma_start(dst[:], w[o * K_PASS : (o + 1) * K_PASS, :].rearrange("(p j) c -> p j c", j=PACK))
+            return dst
 
-        stage = tile([P, T], U8, "stage")
+        stage = tile([P, T], U8, "scale_stage")
 
+        def load_scale_rows(queue, o, q):
+            p0 = 32 * q + 4 * o
+            queue.dma_start(stage[p0 : p0 + 4, :].bitcast(I32), x_scales[o, 4 * q : 4 * q + 4, :].bitcast(I32))
+
+        scale_rows = [(o, q) for q in range(4) for o in range(2)]
         offs_t = load_list(offs, "offs_t")
-        for q in range(4):
-            queue = nc.sync if q < 2 else nc.scalar
-            queue.dma_start(stage[32 * q : 32 * q + 8, :].bitcast(I32), x_scales[:, 4 * q : 4 * q + 4, :].bitcast(I32))
-        w1_0 = load_rows(w1, 0, 0, 512, "w1_0")
-        xw0 = load_words(0)
-        xw1 = load_words(1)
-        w1_1a = load_rows(w1, 1, 0, 256, "w1_1a")
-        w1_1b = load_rows(w1, 1, 256, 256, "w1_1b")
+        for i, (o, q) in enumerate(scale_rows[:5]):
+            load_scale_rows(nc.scalar if i < 3 else nc.sync, o, q)
+        x_window0 = load_words(0)
+        w1_raw0 = load_rows(w1, 0, "w1_raw0")
+        for o, q in scale_rows[5:]:
+            load_scale_rows(nc.sync, o, q)
+        w1_raw1 = load_rows(w1, 1, "w1_raw1")
+        x_window1 = load_words(1)
         unit_t = tile([P, PACK], F32, "unit_t")
         nc.sync.dma_start(unit_t[:], unit.rearrange("(p t) o -> p (t o)", t=PACK))
         lef_t = load_list(lef, "lef_t")
+        w2_raw0 = load_rows(w2, 0, "w2_raw0")
         rig_t = load_list(rig, "rig_t")
+        w2_raw1 = load_rows(w2, 1, "w2_raw1")
         mid_t = load_list(mid, "mid_t")
-        w2_h = [[load_rows(w2, o, 256 * h, 256, "w2_%d%d" % (o, h)) for h in range(2)] for o in range(PASSES)]
-        w3_t = load_rows(w3, 0, 0, N, "w3_t")
+        w3_raw = load_rows(w3, 0, "w3_raw")
 
-        def gather_words(win, o):
-            g = tile([P, S], U32, "xg%d" % o)
-            nc.vector.tensor_copy(g[:], win[:].indirect(offs_t[:]))
-            return g
+        def deal(copy, raw, name, t0, nt):
+            dst = tile([P, nt, P, PACK], BF16, name)
+            copy(dst[:].rearrange("p t m j -> p m j t"), raw[:].rearrange("p j (m t) -> p m j t", t=PACK)[:, :, :, t0 : t0 + nt])
+            return dst
 
-        def deal(copy, raw, name, t0=0, nt=PACK):
-            m = raw.shape[2] // PACK
-            b = tile([P, nt, m, PACK], BF16, name)
-            copy(b[:].rearrange("p t m j -> p m j t"), raw[:].rearrange("p j (m t) -> p m j t", t=PACK)[:, :, :, t0 : t0 + nt])
-            return b
-
-        def planes(width, name):
-            return tile([P, width], U32, name + "_c"), tile([P, width], U8, name + "_s")
-
-        def quant(cs, c0, src):
+        def quantize(src, name):
             n = src.shape[1] // PACK
-            nc.vector.quantize_mx(cs[0][:, c0 : c0 + n].bitcast(FP8X4), cs[1][:, c0 : c0 + n], src)
+            codes = tile([P, n], U32, name + "_codes")
+            scales = tile([P, n], U8, name + "_scales")
+            nc.vector.quantize_mx(codes[:].bitcast(FP8X4), scales[:], src)
+            return codes, scales
 
-        def first_product(bank, wq, xg, o, t):
-            cols = slice(t * P, (t + 1) * P)
-            nc.tensor.matmul_mx(bank[:], lhsT=wq[0][:, cols].bitcast(FP8X4), lhsT_scale=wq[1][:, cols],
-                                rhs=xg[:].bitcast(FP8X4), rhs_scale=xs[4 * o : P, :],
-                                start=(o == 0), stop=(o == PASSES - 1))
+        def quantize_dealt(dealt, name):
+            return quantize(dealt[:].rearrange("p t m j -> p (t m j)"), name)
 
-        y = [tile([P, Y_WIN], F32, "y%d" % t) for t in range(PACK)]
-        z = [tile([P, Z_WIN], F32, "z%d" % t) for t in range(PACK)]
-        for t in range(PACK):
-            nc.gpsimd.memset(y[t][:, S:], 0.0)
-            nc.gpsimd.memset(z[t][:, S:], 0.0)
-        xs_win = tile([P, T], U8, "xs_win")
-        nc.vector.memset(xs_win[:].bitcast(I32), 0)
-        b = deal(nc.scalar.copy, w1_0, "w1_0b")
+        def pier_product(bank, wq, m0, o, c0, n, start, stop):
+            nc.tensor.matmul_mx(bank[:, c0 : c0 + n], lhsT=wq[0][:, m0 : m0 + P].bitcast(FP8X4), lhsT_scale=wq[1][:, m0 : m0 + P],
+                                rhs=x_codes[o][:, c0 : c0 + n].bitcast(FP8X4), rhs_scale=x_scale[4 * o : P, c0 : c0 + n],
+                                start=start, stop=stop)
+
+        y = [tile([P, WINDOW], F32, "y%d" % t) for t in range(PACK)]
+        z = [tile([P, WINDOW], F32, "z%d" % t) for t in range(PACK)]
+        for window in y + z:
+            nc.gpsimd.memset(window[:, S:], 0.0)
+        x_codes = [tile([P, S], U32, "x_codes%d" % o) for o in range(2)]
+        nc.vector.tensor_copy(x_codes[0][:], x_window0[:].indirect(offs_t[:]))
+        scale_window = tile([P, T], U8, "scale_window")
+        nc.vector.memset(scale_window[:].bitcast(I32), 0)
         for q in range(4):
             rows = slice(32 * q, 32 * q + 8)
-            nc.vector.tensor_copy(xs_win[rows, :].bitcast(I32), stage[rows, :].bitcast(I32))
-        xs = tile([P, S], U8, "xs")
-        nc.vector.tensor_copy(xs[:], xs_win[:].indirect(offs_t[:]))
-        xg0 = gather_words(xw0, 0)
-        w1q0 = planes(H, "w1q0")
-        quant(w1q0, 0, b[:].rearrange("p t m j -> p (t m j)"))
-        ybank = [ps.tile([P, S], F32, name="bank%d" % t) for t in range(PACK)]
+            nc.vector.tensor_copy(scale_window[rows, :].bitcast(I32), stage[rows, :].bitcast(I32))
+        x_scale = tile([P, S], U8, "x_scale")
+        nc.vector.tensor_copy(x_scale[:], scale_window[:].indirect(offs_t[:]))
+        w1q0 = quantize_dealt(deal(nc.scalar.copy, w1_raw0, "w1_dealt0", 0, PACK), "w1q0")
+        y_bank = [ps.tile([P, S], F32, name="bank%d" % t) for t in range(PACK)]
         for t in range(PACK):
-            first_product(ybank[t], w1q0, xg0, 0, t)
-        xg1 = gather_words(xw1, 1)
-        w1q1 = planes(H, "w1q1")
-        ba = [deal(nc.vector.tensor_copy, w1_1a, "w1_1a0", 0, 2), deal(nc.scalar.copy, w1_1a, "w1_1a1", 2, 2)]
+            pier_product(y_bank[t], w1q0, t * P, 0, 0, S, True, False)
+        w1_dealt1 = [deal(copy, w1_raw1, "w1_dealt1%d" % h, 2 * h, 2) for h, copy in enumerate((nc.vector.tensor_copy, nc.scalar.copy))]
+        w1q1 = [quantize_dealt(w1_dealt1[h], "w1q1%d" % h) for h in range(2)]
+        for h in range(2):
+            nc.vector.tensor_copy(x_codes[1][:, h * 256 : (h + 1) * 256], x_window1[:].indirect(offs_t[:, h * 16 : (h + 1) * 16]))
+        for h in range(2):
+            for t in range(PACK):
+                pier_product(y_bank[t], w1q1[t // 2], (t % 2) * P, 1, h * 256, 256, False, h == 1)
         for t in range(PACK):
-            quant(w1q1, t * P, ba[t // 2][:, t % 2, :, :].rearrange("p m j -> p (m j)"))
-        bb = [deal(nc.vector.tensor_copy, w1_1b, "w1_1b0", 0, 2), deal(nc.scalar.copy, w1_1b, "w1_1b1", 2, 2)]
-        for t in range(PACK):
-            quant(w1q1, t * P + 64, bb[t // 2][:, t % 2, :, :].rearrange("p m j -> p (m j)"))
-            first_product(ybank[t], w1q1, xg1, 1, t)
-        for t in range(PACK):
-            if t != 7:
-                nc.scalar.activation(y[t][:, :S], ybank[t][:], COPY, scale=unit_t[:, t : t + 1])
+            if t in Y_ON_VECTOR:
+                nc.vector.tensor_scalar(y[t][:, :S], y_bank[t][:], unit_t[:, t : t + 1], None, MULT)
             else:
-                nc.vector.tensor_scalar(y[t][:, :S], ybank[t][:], unit_t[:, t : t + 1], None, MULT)
+                nc.scalar.activation(y[t][:, :S], y_bank[t][:], COPY, scale=unit_t[:, t : t + 1])
 
-        def entries(lst, c):
-            c0, n = CHUNKS[c]
-            return lst[:, c0 // 16 : (c0 + n) // 16]
+        z_bank = [ps.tile([P, S], F32, name="bank%d" % (PACK + t)) for t in range(PACK)]
+        w2_dealt0 = [deal(nc.vector.tensor_copy, w2_raw0, "w2_dealt0%d" % h, 2 * h, 2) for h in range(2)]
+        w2q0 = [quantize_dealt(w2_dealt0[h], "w2q0%d" % h) for h in range(2)]
+        for t in range(PACK):
+            pier_product(z_bank[t], w2q0[t // 2], (t % 2) * P, 0, 0, S, True, False)
+        w2_dealt1 = [deal(nc.vector.tensor_copy, w2_raw1, "w2_dealt1%d" % h, 2 * h, 2) for h in range(2)]
+        w2q1 = [quantize_dealt(w2_dealt1[h], "w2q1%d" % h) for h in range(2)]
+        for t in range(PACK):
+            pier_product(z_bank[t], w2q1[t // 2], (t % 2) * P, 1, 0, S, False, True)
+        for t in range(PACK):
+            nc.scalar.copy(z[t][:, :S], z_bank[t][:])
 
         left = tile([P, PACK, U], F32, "left")
-        prod = tile([P, PACK, U], F32, "prod")
-
-        def g_left(t):
+        ends_t = tile([P, PACK, U], F32, "ends", "w2_dealt11")
+        ends = [ends_t[:, t, :] for t in range(PACK)]
+        for t in range(PACK):
             nc.scalar.activation(left[:, t, :], y[t][:].indirect(lef_t[:]), COPY)
+            nc.vector.tensor_tensor(ends[t], y[t][:].indirect(rig_t[:]), left[:, t, :], ADD)
 
-        def g_ends(t):
-            nc.vector.tensor_tensor(ends[:, t, :], y[t][:].indirect(rig_t[:]), left[:, t, :], ADD)
+        w3_bf = tile([P, N, PACK], BF16, "w3_bf")
+        nc.vector.tensor_copy(w3_bf[:].rearrange("p (c i) j -> p c j i", i=4), w3_raw[:].rearrange("p j (c i) -> p c j i", i=4))
+        stiff = tile([P, U], F32, "stiff")
+        nc.scalar.activation(stiff[:], z[PACK - 1][:].indirect(mid_t[:]), COPY)
+        prod = tile([P, PACK, U], F32, "prod")
+        for t in range(PACK - 1):
+            nc.vector.tensor_tensor(prod[:, t, :], z[t][:].indirect(mid_t[:]), ends[t], MULT)
+        nc.vector.tensor_tensor(prod[:, PACK - 1, :], stiff[:], ends[PACK - 1], MULT)
 
-        def g_load(c):
-            c0, n = LOADS[c]
+        load_head = tile([P, PACK * 512], F32, "load_head", "w2q11_codes")
+        load_tail = tile([P, PACK * 512], F32, "load_tail", "w2q11_scales")
+        load = [view.rearrange("p (t n) -> p t n", t=PACK) for view in (load_head[:], load_tail[:, : PACK * 256], load_tail[:, PACK * 256 : PACK * 384], load_tail[:, PACK * 384 :])]
+        for piece, (c0, n) in enumerate(PIECES):
             for t in range(PACK):
-                nc.scalar.activation(load[c][:, t, :], y[t][:].indirect(mid_t[:, c0 // 16 : (c0 + n) // 16]), COPY)
+                nc.scalar.activation(load[piece][:, t, :], y[t][:].indirect(mid_t[:, c0 // 16 : (c0 + n) // 16]), COPY)
 
-        def g_prod(c):
-            for t in range(PACK):
-                nc.vector.tensor_tensor(prod[:, t, :ZS], z[t][:].indirect(entries(mid_t, c)), ends[:, t, CHUNKS[c][0] : CHUNKS[c][0] + CHUNKS[c][1]], MULT)
-
-        def g_stiff(c):
-            st = tile([P, PACK, CHUNKS[c][1]], F32, "stiff")
-            for t in range(PACK):
-                nc.scalar.activation(st[:, t, :], z[t][:].indirect(entries(mid_t, c)), COPY)
-            return st
-
-        def finish(c, a, n, ld):
-            hid = tile([P, n, PACK], BF16, "hid%d_%d" % (c, a))
+        def hidden(piece, a, n):
+            c0 = PIECES[piece][0] + a
+            hid = tile([P, n, PACK], BF16, "hid%d" % c0)
             nc.vector.tensor_tensor(hid[:].rearrange("p (c i) t -> p c t i", i=4),
-                                    prod[:, :, a : a + n].rearrange("p t (c i) -> p c t i", i=4),
-                                    ld.rearrange("p t (c i) -> p c t i", i=4), ADD)
+                                    prod[:, :, c0 : c0 + n].rearrange("p t (c i) -> p c t i", i=4),
+                                    load[piece][:, :, a : a + n].rearrange("p t (c i) -> p c t i", i=4), ADD)
             return hid
 
-        def last_product(c, a, n, hid, b):
-            c0 = a
-            hq = planes(n, "hq%d_%d" % (c, a))
-            quant(hq, 0, hid[:].rearrange("p n t -> p (n t)"))
-            bank = ps.tile([P, S], F32, name="bank%d" % b)
-            for a in range(0, n, 256):
-                cols = slice(a, min(a + 256, n))
-                nc.tensor.matmul_mx(bank[:, cols], lhsT=w3q[0][:].bitcast(FP8X4), lhsT_scale=w3q[1][:],
-                                    rhs=hq[0][:, cols].bitcast(FP8X4), rhs_scale=hq[1][:, cols], start=True, stop=True)
-            res = tile([P, n], F32, "res%d" % b)
-            nc.scalar.copy(res[:], bank[:, 0:n])
+        def modes(bank, a, hid, name):
+            codes, scales = quantize(hid[:].rearrange("p n t -> p (n t)"), name)
+            n = hid.shape[1]
+            for b in range(0, n, 256):
+                cols = slice(b, min(b + 256, n))
+                nc.tensor.matmul_mx(bank[:, a + cols.start : a + cols.stop], lhsT=w3q[0][:].bitcast(FP8X4), lhsT_scale=w3q[1][:],
+                                    rhs=codes[:, cols].bitcast(FP8X4), rhs_scale=scales[:, cols], start=True, stop=True)
+
+        def store(piece, bank, copy):
+            c0, n = PIECES[piece]
+            res = tile([P, n], F32, "res%d" % piece)
+            copy(res[:], bank[:, 0:n])
             nc.sync.dma_start(out[:, c0 : c0 + n], res[:])
 
-        zbank = [ps.tile([P, S], F32, name="bank%d" % (PACK + t)) for t in range(PACK)]
-
-        def deal_halves(o):
-            b = tile([P, PACK, P, PACK], BF16, "w2b%d" % o)
-            for h in range(2):
-                nc.vector.tensor_copy(b[:, :, 64 * h : 64 * h + 64, :].rearrange("p t m j -> p m j t"),
-                                      w2_h[o][h][:].rearrange("p j (m t) -> p m j t", t=PACK))
-            return b
-
-        b20 = deal_halves(0)
-        w2q0 = planes(H, "w2q0")
-        quant(w2q0, 0, b20[:].rearrange("p t m j -> p (t m j)"))
-        for t in range(PACK):
-            first_product(zbank[t], w2q0, xg0, 0, t)
-        b21 = deal_halves(1)
-        w2q1 = [planes(2 * P, "w2q1%d" % h) for h in range(2)]
+        out_bank = [ps.tile([P, S], F32, name="bank%d" % piece) for piece in range(len(PIECES))]
+        halves = [hidden(0, 0, 256), hidden(0, 256, 256)]
+        w3q = quantize(w3_bf[:].rearrange("p n j -> p (n j)"), "w3q")
         for h in range(2):
-            quant(w2q1[h], 0, b21[:, 2 * h : 2 * h + 2, :, :].rearrange("p t m j -> p (t m j)"))
-        for t in range(PACK):
-            first_product(zbank[t], w2q1[t // 2], xg1, 1, t % 2)
-        for t in range(PACK):
-            nc.scalar.copy(z[t][:, :S], zbank[t][:])
-        ends = tile([P, PACK, U], F32, "ends", "w2b1")
-        load_head = tile([P, PACK, 640], F32, "load_head", "w2q11_c")
-        load_tail = tile([P, PACK * 384], F32, "load_tail", "w2q11_s")
-        load = [load_head[:], load_tail[:, : PACK * 256].rearrange("p (t n) -> p t n", t=PACK),
-                load_tail[:, PACK * 256 :].rearrange("p (t n) -> p t n", t=PACK)]
-        for t in range(PACK):
-            g_left(t)
-            g_ends(t)
-        w3b = tile([P, N, PACK], BF16, "w3b", "w2q10_c")
-        nc.scalar.copy(w3b[:].rearrange("p (c i) j -> p c j i", i=4), w3_t[:].rearrange("p j (c i) -> p c j i", i=4))
-        g_load(0)
-        g_prod(0)
-        w3q = planes(N, "w3q")
-        quant(w3q, 0, w3b[:].rearrange("p n j -> p (n j)"))
-        st = g_stiff(1)
-        hid0 = finish(0, 0, 384, load[0][:, :, 0:384])
-        hid1 = finish(0, 384, 256, load[0][:, :, 384:640])
-        last_product(0, 0, 384, hid0, 0)
-        last_product(0, 384, 256, hid1, 1)
-        g_load(1)
-        g_load(2)
-        nc.vector.tensor_tensor(prod[:, :, ZS:], st[:], ends[:, :, CHUNKS[1][0] :], MULT)
-        hid2 = finish(1, 640, 256, load[1])
-        hid3 = finish(1, 896, 128, load[2])
-        last_product(1, 640, 256, hid2, 2)
-        last_product(1, 896, 128, hid3, 3)
+            modes(out_bank[0], 256 * h, halves[h], "hq0%d" % h)
+        store(0, out_bank[0], nc.scalar.copy)
+        rest = [hidden(piece, 0, PIECES[piece][1]) for piece in (1, 2)]
+        modes(out_bank[1], 0, rest[0], "hq1")
+        store(1, out_bank[1], nc.scalar.copy)
+        last = hidden(3, 0, PIECES[3][1])
+        modes(out_bank[2], 0, rest[1], "hq2")
+        store(2, out_bank[2], nc.scalar.copy)
+        modes(out_bank[3], 0, last, "hq3")
+        store(3, out_bank[3], nc.vector.tensor_copy)

from contextlib import ExitStack

import concourse.mybir as mybir

K, T, S, N, H, U = 1024, 2048, 512, 128, 512, 1024
FLOPS = 2 * K * H * S * 2 + 2 * H * N * U

F32 = mybir.dt.float32
BF16 = mybir.dt.bfloat16
I32 = mybir.dt.int32
U32 = mybir.dt.uint32
U16 = mybir.dt.uint16
U8 = mybir.dt.uint8
FP8X4 = mybir.dt.float8_e4m3fn_x4
COPY = mybir.ActivationFunctionType.Copy
ADD = mybir.AluOpType.add
MULT = mybir.AluOpType.mult

P = 128
PACK = 4
K_PASS = P * PACK
WINDOW = U + 16
PIECES = ((0, 512), (512, 256), (768, 128), (896, 128))
Y_ON_VECTOR = (1,)


def tile_picked_ybrdgep_mul_p_kernel(tc, x_words, x_scales, w1, w2, unit, w3, offs, lef, rig, mid, out):
    nc = tc.nc
    with ExitStack() as ctx:
        sb = ctx.enter_context(tc.tile_pool(name="sb", bufs=1))
        ps = ctx.enter_context(tc.psum_pool(name="ps", bufs=1))

        def tile(shape, dtype, name, tag=None):
            return sb.tile(shape, dtype, name=name, tag=tag or name, align_bytes=64)

        def load_list(src, name):
            dst = tile([P, src.shape[1]], U16, name)
            nc.sync.dma_start(dst[:], src)
            return dst

        def load_words(o):
            dst = tile([P, T], U32, "x_window%d" % o)
            nc.sync.dma_start(dst[:].bitcast(I32), x_words[o].rearrange("p n r -> p (n r)").bitcast(I32))
            return dst

        def load_rows(w, o, name):
            dst = tile([P, PACK, w.shape[1]], F32, name)
            nc.sync.dma_start(dst[:], w[o * K_PASS : (o + 1) * K_PASS, :].rearrange("(p j) c -> p j c", j=PACK))
            return dst

        stage = tile([P, T], U8, "scale_stage")

        def load_scale_rows(queue, o, q):
            p0 = 32 * q + 4 * o
            queue.dma_start(stage[p0 : p0 + 4, :].bitcast(I32), x_scales[o, 4 * q : 4 * q + 4, :].bitcast(I32))

        scale_rows = [(o, q) for q in range(4) for o in range(2)]
        offs_t = load_list(offs, "offs_t")
        for i, (o, q) in enumerate(scale_rows[:5]):
            load_scale_rows(nc.scalar if i < 3 else nc.sync, o, q)
        x_window0 = load_words(0)
        w1_raw0 = load_rows(w1, 0, "w1_raw0")
        for o, q in scale_rows[5:]:
            load_scale_rows(nc.sync, o, q)
        w1_raw1 = load_rows(w1, 1, "w1_raw1")
        x_window1 = load_words(1)
        unit_t = tile([P, PACK], F32, "unit_t")
        nc.sync.dma_start(unit_t[:], unit.rearrange("(p t) o -> p (t o)", t=PACK))
        lef_t = load_list(lef, "lef_t")
        w2_raw0 = load_rows(w2, 0, "w2_raw0")
        rig_t = load_list(rig, "rig_t")
        w2_raw1 = load_rows(w2, 1, "w2_raw1")
        mid_t = load_list(mid, "mid_t")
        w3_raw = load_rows(w3, 0, "w3_raw")

        def deal(copy, raw, name, t0, nt):
            dst = tile([P, nt, P, PACK], BF16, name)
            copy(dst[:].rearrange("p t m j -> p m j t"), raw[:].rearrange("p j (m t) -> p m j t", t=PACK)[:, :, :, t0 : t0 + nt])
            return dst

        def quantize(src, name):
            n = src.shape[1] // PACK
            codes = tile([P, n], U32, name + "_codes")
            scales = tile([P, n], U8, name + "_scales")
            nc.vector.quantize_mx(codes[:].bitcast(FP8X4), scales[:], src)
            return codes, scales

        def quantize_dealt(dealt, name):
            return quantize(dealt[:].rearrange("p t m j -> p (t m j)"), name)

        def pier_product(bank, wq, m0, o, c0, n, start, stop):
            nc.tensor.matmul_mx(bank[:, c0 : c0 + n], lhsT=wq[0][:, m0 : m0 + P].bitcast(FP8X4), lhsT_scale=wq[1][:, m0 : m0 + P],
                                rhs=x_codes[o][:, c0 : c0 + n].bitcast(FP8X4), rhs_scale=x_scale[4 * o : P, c0 : c0 + n],
                                start=start, stop=stop)

        y = [tile([P, WINDOW], F32, "y%d" % t) for t in range(PACK)]
        z = [tile([P, WINDOW], F32, "z%d" % t) for t in range(PACK)]
        for window in y + z:
            nc.gpsimd.memset(window[:, S:], 0.0)
        x_codes = [tile([P, S], U32, "x_codes%d" % o) for o in range(2)]
        nc.vector.tensor_copy(x_codes[0][:], x_window0[:].indirect(offs_t[:]))
        scale_window = tile([P, T], U8, "scale_window")
        nc.vector.memset(scale_window[:].bitcast(I32), 0)
        for q in range(4):
            rows = slice(32 * q, 32 * q + 8)
            nc.vector.tensor_copy(scale_window[rows, :].bitcast(I32), stage[rows, :].bitcast(I32))
        x_scale = tile([P, S], U8, "x_scale")
        nc.vector.tensor_copy(x_scale[:], scale_window[:].indirect(offs_t[:]))
        w1q0 = quantize_dealt(deal(nc.scalar.copy, w1_raw0, "w1_dealt0", 0, PACK), "w1q0")
        y_bank = [ps.tile([P, S], F32, name="bank%d" % t) for t in range(PACK)]
        for t in range(PACK):
            pier_product(y_bank[t], w1q0, t * P, 0, 0, S, True, False)
        w1_dealt1 = [deal(copy, w1_raw1, "w1_dealt1%d" % h, 2 * h, 2) for h, copy in enumerate((nc.vector.tensor_copy, nc.scalar.copy))]
        w1q1 = [quantize_dealt(w1_dealt1[h], "w1q1%d" % h) for h in range(2)]
        for h in range(2):
            nc.vector.tensor_copy(x_codes[1][:, h * 256 : (h + 1) * 256], x_window1[:].indirect(offs_t[:, h * 16 : (h + 1) * 16]))
        for h in range(2):
            for t in range(PACK):
                pier_product(y_bank[t], w1q1[t // 2], (t % 2) * P, 1, h * 256, 256, False, h == 1)
        for t in range(PACK):
            if t in Y_ON_VECTOR:
                nc.vector.tensor_scalar(y[t][:, :S], y_bank[t][:], unit_t[:, t : t + 1], None, MULT)
            else:
                nc.scalar.activation(y[t][:, :S], y_bank[t][:], COPY, scale=unit_t[:, t : t + 1])

        z_bank = [ps.tile([P, S], F32, name="bank%d" % (PACK + t)) for t in range(PACK)]
        w2_dealt0 = [deal(nc.vector.tensor_copy, w2_raw0, "w2_dealt0%d" % h, 2 * h, 2) for h in range(2)]
        w2q0 = [quantize_dealt(w2_dealt0[h], "w2q0%d" % h) for h in range(2)]
        for t in range(PACK):
            pier_product(z_bank[t], w2q0[t // 2], (t % 2) * P, 0, 0, S, True, False)
        w2_dealt1 = [deal(nc.vector.tensor_copy, w2_raw1, "w2_dealt1%d" % h, 2 * h, 2) for h in range(2)]
        w2q1 = [quantize_dealt(w2_dealt1[h], "w2q1%d" % h) for h in range(2)]
        for t in range(PACK):
            pier_product(z_bank[t], w2q1[t // 2], (t % 2) * P, 1, 0, S, False, True)
        for t in range(PACK):
            nc.scalar.copy(z[t][:, :S], z_bank[t][:])

        left = tile([P, PACK, U], F32, "left")
        ends_t = tile([P, PACK, U], F32, "ends", "w2_dealt11")
        ends = [ends_t[:, t, :] for t in range(PACK)]
        for t in range(PACK):
            nc.scalar.activation(left[:, t, :], y[t][:].indirect(lef_t[:]), COPY)
            nc.vector.tensor_tensor(ends[t], y[t][:].indirect(rig_t[:]), left[:, t, :], ADD)

        w3_bf = tile([P, N, PACK], BF16, "w3_bf")
        nc.vector.tensor_copy(w3_bf[:].rearrange("p (c i) j -> p c j i", i=4), w3_raw[:].rearrange("p j (c i) -> p c j i", i=4))
        stiff = tile([P, U], F32, "stiff")
        nc.scalar.activation(stiff[:], z[PACK - 1][:].indirect(mid_t[:]), COPY)
        prod = tile([P, PACK, U], F32, "prod")
        for t in range(PACK - 1):
            nc.vector.tensor_tensor(prod[:, t, :], z[t][:].indirect(mid_t[:]), ends[t], MULT)
        nc.vector.tensor_tensor(prod[:, PACK - 1, :], stiff[:], ends[PACK - 1], MULT)

        load_head = tile([P, PACK * 512], F32, "load_head", "w2q11_codes")
        load_tail = tile([P, PACK * 512], F32, "load_tail", "w2q11_scales")
        load = [view.rearrange("p (t n) -> p t n", t=PACK) for view in (load_head[:], load_tail[:, : PACK * 256], load_tail[:, PACK * 256 : PACK * 384], load_tail[:, PACK * 384 :])]
        for piece, (c0, n) in enumerate(PIECES):
            for t in range(PACK):
                nc.scalar.activation(load[piece][:, t, :], y[t][:].indirect(mid_t[:, c0 // 16 : (c0 + n) // 16]), COPY)

        def hidden(piece, a, n):
            c0 = PIECES[piece][0] + a
            hid = tile([P, n, PACK], BF16, "hid%d" % c0)
            nc.vector.tensor_tensor(hid[:].rearrange("p (c i) t -> p c t i", i=4),
                                    prod[:, :, c0 : c0 + n].rearrange("p t (c i) -> p c t i", i=4),
                                    load[piece][:, :, a : a + n].rearrange("p t (c i) -> p c t i", i=4), ADD)
            return hid

        def modes(bank, a, hid, name):
            codes, scales = quantize(hid[:].rearrange("p n t -> p (n t)"), name)
            n = hid.shape[1]
            for b in range(0, n, 256):
                cols = slice(b, min(b + 256, n))
                nc.tensor.matmul_mx(bank[:, a + cols.start : a + cols.stop], lhsT=w3q[0][:].bitcast(FP8X4), lhsT_scale=w3q[1][:],
                                    rhs=codes[:, cols].bitcast(FP8X4), rhs_scale=scales[:, cols], start=True, stop=True)

        def store(piece, bank, copy):
            c0, n = PIECES[piece]
            res = tile([P, n], F32, "res%d" % piece)
            copy(res[:], bank[:, 0:n])
            nc.sync.dma_start(out[:, c0 : c0 + n], res[:])

        out_bank = [ps.tile([P, S], F32, name="bank%d" % piece) for piece in range(len(PIECES))]
        halves = [hidden(0, 0, 256), hidden(0, 256, 256)]
        w3q = quantize(w3_bf[:].rearrange("p n j -> p (n j)"), "w3q")
        for h in range(2):
            modes(out_bank[0], 256 * h, halves[h], "hq0%d" % h)
        store(0, out_bank[0], nc.scalar.copy)
        rest = [hidden(piece, 0, PIECES[piece][1]) for piece in (1, 2)]
        modes(out_bank[1], 0, rest[0], "hq1")
        store(1, out_bank[1], nc.scalar.copy)
        last = hidden(3, 0, PIECES[3][1])
        modes(out_bank[2], 0, rest[1], "hq2")
        store(2, out_bank[2], nc.scalar.copy)
        modes(out_bank[3], 0, last, "hq3")
        store(3, out_bank[3], nc.vector.tensor_copy)
